import numpy as np
import ml_dtypes


def mxq(x, axis, fmt="e4m3"):
    dtype, down = {"e4m3": (ml_dtypes.float8_e4m3fn, 7), "e5m2": (ml_dtypes.float8_e5m2, 14)}[fmt]
    v = np.moveaxis(np.asarray(x, np.float32).astype(ml_dtypes.bfloat16).astype(np.float64), axis, -1)
    blocks = v.reshape(v.shape[:-1] + (-1, 32))
    amax = np.abs(blocks).max(-1, keepdims=True)
    byte = np.maximum(np.where(amax > 0, np.frexp(amax)[1] - 1 + 127, 0) - down, 1)
    scale = np.exp2(byte - 127.0)
    codes = (blocks / scale).astype(np.float32).astype(dtype).astype(np.float64)
    return np.moveaxis((codes * scale).reshape(v.shape), -1, axis)


WIDE = False


def mx_kscale(k):
    if not WIDE:
        return np.ones(k)
    levels = np.array([10, -10, 5, -5, 0])
    if k % 512:
        return np.exp2(np.random.permutation(np.resize(levels, k // 32))).repeat(32)
    a = np.empty((k // 512, 16))
    for p in range(k // 512):
        a[p, :8] = np.random.permutation(np.resize(levels, 8))
        for g in range(8):
            far = levels[np.abs(levels - a[p, g]) >= 10]
            a[p, g + 8] = far[np.random.randint(len(far))]
    return np.exp2(a.ravel()).repeat(32)


def f64(x):
    return np.asarray(x).astype(np.float64)


def striped8(idx):
    return np.asarray(idx).reshape(8, -1, 16).transpose(0, 2, 1).reshape(128, -1).astype(np.uint16)


def unstriped8(offs):
    return offs.reshape(8, 16, -1).transpose(0, 2, 1).reshape(8, -1).astype(np.int64)


def pick8(x, idx, run):
    r = np.arange(len(x))
    return x[r[:, None], idx[r % (8 * run) // run]]


E2M1 = np.array([0.0, 0.5, 1.0, 1.5, 2.0, 3.0, 4.0, 6.0, -0.0, -0.5, -1.0, -1.5, -2.0, -3.0, -4.0, -6.0])


def pack_weight(w, fmt):
    k, n = w.shape
    w = f64(np.asarray(w, np.float32).astype(ml_dtypes.bfloat16)).reshape(k // 32, 32, n)
    amax = np.abs(w).max(1)
    if fmt == "e4m3":
        byte = np.frexp(amax)[1] - 1 + 127 - 7
    else:
        mant, ex = np.frexp(amax / 6.0)
        byte = np.where(mant > 0.5, ex, ex - 1) + 127
    byte = np.clip(np.where(amax > 0, byte, 1), 1, 254)
    scaled = (w * np.exp2(127.0 - byte)[:, None, :]).reshape(k, n).astype(np.float32)
    by_word = np.ascontiguousarray(scaled.reshape(k // 512, 128, 4, n).transpose(0, 1, 3, 2))
    if fmt == "e4m3":
        words = by_word.astype(ml_dtypes.float8_e4m3fn).view(np.uint8)
    else:
        c = by_word.astype(ml_dtypes.float4_e2m1fn).view(np.uint8) & 0xF
        words = (c[..., 0::2] | (c[..., 1::2] << 4)).reshape(k // 512, 128, 2 * n)
    return np.ascontiguousarray(words), np.ascontiguousarray(byte.astype(np.uint8).reshape(k // 512, 16, n))


def unpack_weight(words, scales, fmt):
    g, _, n = scales.shape
    words = np.ascontiguousarray(words).reshape(g, 128, n, -1)
    if fmt == "e4m3":
        vals = words.view(ml_dtypes.float8_e4m3fn).astype(np.float64)
    else:
        nib = np.empty((g, 128, n, 4), np.uint8)
        nib[..., 0::2] = words & 0xF
        nib[..., 1::2] = words >> 4
        vals = E2M1[nib]
    vals = vals * np.repeat(np.exp2(scales.astype(np.float64) - 127.0), 8, axis=1)[..., None]
    return vals.transpose(0, 1, 3, 2).reshape(g * 512, n)


K, T, J, L, N = 512, 1024, 512, 512, 512


def setup_inputs():
    n = np.random.standard_normal
    idx = np.stack([np.random.permutation(T)[:J] for _ in range(8)])
    fk = mx_kscale(K)
    fl = mx_kscale(L)
    wp = pack_weight(n((K, N)) * 1 / np.sqrt(K) * fk[:, None], "e2m1")
    cxp = pack_weight(n((L, J)) / fl[:, None], "e4m3")
    wcp = pack_weight(n((L, N)) * 1 / np.sqrt(L) * fl[:, None], "e2m1")
    return {
        "xf": (n((K, T))).astype(np.float32),
        "fk": (np.random.uniform(0.5, 2.0, (K, 1)) / fk[:, None]).astype(np.float32),
        "w_words": wp[0],
        "w_scales": wp[1],
        "cx_words": cxp[0],
        "cx_scales": cxp[1],
        "wc_words": wcp[0],
        "wc_scales": wcp[1],
        "offs": striped8(idx),
    }


def reference(xf, fk, w_words, w_scales, cx_words, cx_scales, wc_words, wc_scales, offs):
    idx = unstriped8(offs)
    wu = unpack_weight(w_words, w_scales, "e2m1")
    cxu = unpack_weight(cx_words, cx_scales, "e4m3")
    wcu = unpack_weight(wc_words, wc_scales, "e2m1")
    xs = pick8(f64(xf), idx, 64) * f64(fk)
    xsq = mxq(xs, 0, "e4m3")
    p = wu.T @ xsq
    q = wcu.T @ cxu
    y = np.maximum(p, 0.0) + q
    return y

@@ -1,0 +1,136 @@
+from contextlib import ExitStack
+
+import concourse.mybir as mybir
+
+K, T, J, L, N = 512, 1024, 512, 512, 512
+FLOPS = 2 * K * N * J + 2 * L * N * J
+
+F32 = mybir.dt.float32
+BF16 = mybir.dt.bfloat16
+I32 = mybir.dt.int32
+U32 = mybir.dt.uint32
+U16 = mybir.dt.uint16
+U8 = mybir.dt.uint8
+FP8X4 = mybir.dt.float8_e4m3fn_x4
+FP4X4 = mybir.dt.float4_e2m1fn_x4
+COPY = mybir.ActivationFunctionType.Copy
+MAX = mybir.AluOpType.max
+ADD = mybir.AluOpType.add
+
+P = 128
+PACK = 4
+HALF = J // 2
+LIST_COLS = HALF // 16
+
+
+def tile_list_group_picks_and_context_kernel(
+    tc, xf, fk, w_words, w_scales, cx_words, cx_scales, wc_words, wc_scales, offs, out
+):
+    nc = tc.nc
+    with ExitStack() as ctx:
+        keep = ctx.enter_context(tc.tile_pool(name="keep", bufs=1))
+        psum = ctx.enter_context(tc.psum_pool(name="psum", bufs=1))
+
+        offsets = keep.tile([P, J // 16], U16, name="offsets")
+        factor = keep.tile([P, PACK], F32, name="factor")
+        planes = [keep.tile([P, T], F32, name="plane%d" % t) for t in range(PACK)]
+        w_codes = keep.tile([P, 2 * N], U8, name="w_codes", align_bytes=64)
+        wc_codes = keep.tile([P, 2 * N], U8, name="wc_codes", align_bytes=64)
+        cx_codes = keep.tile([P, J], U32, name="cx_codes", align_bytes=64)
+        scale_rows = keep.tile([P, N + N + J], U8, name="scale_rows", align_bytes=64)
+        wc_scale = scale_rows[:, 0:N]
+        cx_scale = scale_rows[:, N : N + J]
+        w_scale = scale_rows[:, N + J : N + J + N]
+        nc.vector.memset(scale_rows[32:64, :].bitcast(I32), 0)
+        nc.vector.memset(scale_rows[64:P, :].bitcast(I32), 0)
+        warm = keep.tile([P, 8], F32, name="warm")
+        warm2 = keep.tile([P, 8], F32, name="warm2")
+        nc.vector.memset(warm[:], 0.0)
+        nc.scalar.activation(out=warm2[:], in_=warm[:], func=COPY)
+
+        xf_rows = xf.rearrange("(p t) c -> p t c", t=PACK)
+        nc.sync.dma_start(out=planes[0][:], in_=xf_rows[:, 0, :])
+        nc.sync.dma_start(offsets[:], offs)
+        nc.sync.dma_start(out=factor[:], in_=fk.rearrange("(p t) o -> p (t o)", t=PACK))
+        for plane, rows in ((wc_scale, wc_scales), (cx_scale, cx_scales), (w_scale, w_scales)):
+            nc.sync.dma_start(out=plane[0:32, :].bitcast(I32), in_=rows[0].bitcast(I32).partition_broadcast(2))
+        for t in range(1, PACK):
+            nc.sync.dma_start(out=planes[t][:], in_=xf_rows[:, t, :])
+        nc.sync.dma_start(out=wc_codes[:].bitcast(I32), in_=wc_words[0].bitcast(I32))
+        nc.sync.dma_start(
+            out=cx_codes[:].bitcast(I32), in_=cx_words[0].rearrange("p c r -> p (c r)").bitcast(I32)
+        )
+        nc.sync.dma_start(out=w_codes[:].bitcast(I32), in_=w_words[0].bitcast(I32))
+        for quad in range(1, 4):
+            nc.scalar.dma_start(
+                out=scale_rows[32 * quad : 32 * quad + 4, :].bitcast(I32),
+                in_=scale_rows[4 * quad : 4 * quad + 4, :].bitcast(I32),
+            )
+
+        pairs = [keep.tile([P, 2, HALF, 2], BF16, name="pairs%d" % h) for h in range(2)]
+
+        def scale_and_round(picked, t, h):
+            nc.scalar.activation(
+                out=pairs[h][:, t // 2, :, t % 2], in_=picked, func=COPY, scale=factor[:, t : t + 1]
+            )
+
+        for t in range(PACK - 1):
+            picked = keep.tile([P, J], F32, name="picked%d" % t)
+            nc.vector.tensor_copy(picked[:], planes[t][:].indirect(offsets[:]))
+            for h in range(2):
+                scale_and_round(picked[:, h * HALF : (h + 1) * HALF], t, h)
+        for h in range(2):
+            picked = keep.tile([P, HALF], F32, name="picked_last%d" % h)
+            nc.vector.tensor_copy(
+                picked[:], planes[PACK - 1][:].indirect(offsets[:, h * LIST_COLS : (h + 1) * LIST_COLS])
+            )
+            scale_and_round(picked[:], PACK - 1, h)
+
+        def product(bank, codes, scale, m, rhs, rhs_scale):
+            for s in range(2):
+                tile_n = 2 * m + s
+                nc.tensor.matmul_mx(
+                    out=bank[:, s, :],
+                    lhsT=codes[:, 2 * P * tile_n : 2 * P * (tile_n + 1)].bitcast(FP4X4),
+                    lhsT_scale=scale[:, P * tile_n : P * (tile_n + 1)],
+                    rhs=rhs.bitcast(FP8X4),
+                    rhs_scale=rhs_scale,
+                    start=True,
+                    stop=True,
+                )
+
+        context = {}
+        for h in range(2):
+            cols = slice(h * HALF, (h + 1) * HALF)
+            for m in range(2):
+                bank = psum.tile([P, 2, HALF], F32, name="q_bank%d%d" % (h, m))
+                product(bank, wc_codes, wc_scale, m, cx_codes[:, cols], cx_scale[:, cols])
+                context[h, m] = keep.tile([P, 2, HALF], F32, name="context%d%d" % (h, m))
+                nc.scalar.copy(out=context[h, m][:], in_=bank[:])
+
+        banks = {}
+        for h in range(2):
+            grouped = keep.tile([P, HALF * PACK], BF16, name="grouped%d" % h, align_bytes=64)
+            nc.vector.tensor_copy(
+                out=grouped[:].bitcast(I32).rearrange("p (c u) -> p c u", u=2),
+                in_=pairs[h][:].rearrange("p u c e -> p u (c e)").bitcast(I32).rearrange("p u c -> p c u"),
+            )
+            xs_codes = keep.tile([P, HALF], U32, name="xs_codes%d" % h, align_bytes=64)
+            xs_scale = keep.tile([P, HALF], U8, name="xs_scale%d" % h, align_bytes=64)
+            nc.vector.quantize_mx(out=xs_codes[:].bitcast(FP8X4), scales=xs_scale[:], in_=grouped[:])
+            for m in range(2):
+                banks[h, m] = psum.tile([P, 2, HALF], F32, name="p_bank%d%d" % (h, m))
+                product(banks[h, m], w_codes, w_scale, m, xs_codes[:], xs_scale[:])
+
+        for h in range(2):
+            for m in range(2):
+                result = keep.tile([P, 2, HALF], F32, name="result%d%d" % (h, m))
+                nc.vector.scalar_tensor_tensor(
+                    out=result[:], in0=banks[h, m][:], scalar=0.0, in1=context[h, m][:], op0=MAX, op1=ADD
+                )
+                nc.sync.dma_start(
+                    out=out[2 * P * m : 2 * P * (m + 1), h * HALF : (h + 1) * HALF].rearrange(
+                        "(s p) j -> p s j", s=2
+                    ),
+                    in_=result[:],
+                )

@@ -34,15 +34,11 @@ def tile_list_group_picks_and_context_kernel(
         offsets = keep.tile([P, J // 16], U16, name="offsets")
         factor = keep.tile([P, PACK], F32, name="factor")
         planes = [keep.tile([P, T], F32, name="plane%d" % t) for t in range(PACK)]
-        w_codes = keep.tile([P, 2 * N], U8, name="w_codes", align_bytes=64)
-        wc_codes = keep.tile([P, 2 * N], U8, name="wc_codes", align_bytes=64)
-        cx_codes = keep.tile([P, J], U32, name="cx_codes", align_bytes=64)
-        scale_rows = keep.tile([P, N + N + J], U8, name="scale_rows", align_bytes=64)
-        wc_scale = scale_rows[:, 0:N]
-        cx_scale = scale_rows[:, N : N + J]
-        w_scale = scale_rows[:, N + J : N + J + N]
-        nc.vector.memset(scale_rows[32:64, :].bitcast(I32), 0)
-        nc.vector.memset(scale_rows[64:P, :].bitcast(I32), 0)
+        scale_rows = keep.tile([16, N + J + N], U8, name="scale_rows")
+        scales = keep.tile([P, N + J + N], U8, name="scales", align_bytes=64)
+        wc_cols, cx_cols, w_cols = slice(0, N), slice(N, N + J), slice(N + J, N + J + N)
+        wc_scale, cx_scale, w_scale = scales[:, wc_cols], scales[:, cx_cols], scales[:, w_cols]
+        nc.vector.memset(scales[:].bitcast(I32), 0)
         warm = keep.tile([P, 8], F32, name="warm")
         warm2 = keep.tile([P, 8], F32, name="warm2")
         nc.vector.memset(warm[:], 0.0)
@@ -52,18 +48,13 @@ def tile_list_group_picks_and_context_kernel(
         nc.sync.dma_start(out=planes[0][:], in_=xf_rows[:, 0, :])
         nc.sync.dma_start(offsets[:], offs)
         nc.sync.dma_start(out=factor[:], in_=fk.rearrange("(p t) o -> p (t o)", t=PACK))
-        for plane, rows in ((wc_scale, wc_scales), (cx_scale, cx_scales), (w_scale, w_scales)):
-            nc.sync.dma_start(out=plane[0:32, :].bitcast(I32), in_=rows[0].bitcast(I32).partition_broadcast(2))
+        for cols, rows in ((wc_cols, wc_scales), (cx_cols, cx_scales), (w_cols, w_scales)):
+            nc.sync.dma_start(out=scale_rows[:, cols].bitcast(I32), in_=rows[0].bitcast(I32))
         for t in range(1, PACK):
             nc.sync.dma_start(out=planes[t][:], in_=xf_rows[:, t, :])
-        nc.sync.dma_start(out=wc_codes[:].bitcast(I32), in_=wc_words[0].bitcast(I32))
-        nc.sync.dma_start(
-            out=cx_codes[:].bitcast(I32), in_=cx_words[0].rearrange("p c r -> p (c r)").bitcast(I32)
-        )
-        nc.sync.dma_start(out=w_codes[:].bitcast(I32), in_=w_words[0].bitcast(I32))
-        for quad in range(1, 4):
-            nc.scalar.dma_start(
-                out=scale_rows[32 * quad : 32 * quad + 4, :].bitcast(I32),
+        for quad in range(4):
+            nc.sync.dma_start(
+                out=scales[32 * quad : 32 * quad + 4, :].bitcast(I32),
                 in_=scale_rows[4 * quad : 4 * quad + 4, :].bitcast(I32),
             )
 
@@ -74,25 +65,41 @@ def tile_list_group_picks_and_context_kernel(
                 out=pairs[h][:, t // 2, :, t % 2], in_=picked, func=COPY, scale=factor[:, t : t + 1]
             )
 
-        for t in range(PACK - 1):
-            picked = keep.tile([P, J], F32, name="picked%d" % t)
-            nc.vector.tensor_copy(picked[:], planes[t][:].indirect(offsets[:]))
+        for t in range(PACK):
             for h in range(2):
-                scale_and_round(picked[:, h * HALF : (h + 1) * HALF], t, h)
-        for h in range(2):
-            picked = keep.tile([P, HALF], F32, name="picked_last%d" % h)
-            nc.vector.tensor_copy(
-                picked[:], planes[PACK - 1][:].indirect(offsets[:, h * LIST_COLS : (h + 1) * LIST_COLS])
-            )
-            scale_and_round(picked[:], PACK - 1, h)
+                picked = keep.tile([P, HALF], F32, name="picked%d%d" % (t, h), align_bytes=64)
+                nc.vector.tensor_copy(
+                    picked[:], planes[t][:].indirect(offsets[:, h * LIST_COLS : (h + 1) * LIST_COLS])
+                )
+                scale_and_round(picked[:], t, h)
 
-        def product(bank, codes, scale, m, rhs, rhs_scale):
+        xs_codes, xs_scale = {}, {}
+        for h in range(2):
+            grouped = keep.tile([P, HALF * PACK], BF16, name="grouped%d" % h, align_bytes=64)
+            nc.vector.tensor_copy(
+                out=grouped[:].bitcast(F32).rearrange("p (c i u) -> p c u i", i=4, u=2),
+                in_=pairs[h][:].rearrange("p u c e -> p u (c e)").bitcast(F32).rearrange("p u (c i) -> p c u i", i=4),
+            )
+            xs_codes[h] = keep.tile([P, HALF], U32, name="xs_codes%d" % h, align_bytes=64)
+            xs_scale[h] = keep.tile([P, HALF], U8, name="xs_scale%d" % h, align_bytes=64)
+            nc.vector.quantize_mx(out=xs_codes[h][:].bitcast(FP8X4), scales=xs_scale[h][:], in_=grouped[:])
+
+        codes = keep.tile([P, 2 * N + 4 * J + 2 * N], U8, name="codes", tag="picked00", align_bytes=64)
+        wc_codes, w_codes = codes[:, 0 : 2 * N], codes[:, 2 * N : 4 * N]
+        cx_codes = [codes[:, 4 * N + 4 * HALF * h : 4 * N + 4 * HALF * (h + 1)] for h in range(2)]
+        cx_rows = cx_words[0].rearrange("p c r -> p (c r)")
+        nc.sync.dma_start(out=wc_codes.bitcast(I32), in_=wc_words[0].bitcast(I32))
+        nc.sync.dma_start(out=cx_codes[0].bitcast(I32), in_=cx_rows[:, 0 : 4 * HALF].bitcast(I32))
+        nc.sync.dma_start(out=cx_codes[1].bitcast(I32), in_=cx_rows[:, 4 * HALF : 4 * J].bitcast(I32))
+        nc.sync.dma_start(out=w_codes.bitcast(I32), in_=w_words[0].bitcast(I32))
+
+        def product(bank, weight, weight_scale, m, rhs, rhs_scale):
             for s in range(2):
                 tile_n = 2 * m + s
                 nc.tensor.matmul_mx(
                     out=bank[:, s, :],
-                    lhsT=codes[:, 2 * P * tile_n : 2 * P * (tile_n + 1)].bitcast(FP4X4),
-                    lhsT_scale=scale[:, P * tile_n : P * (tile_n + 1)],
+                    lhsT=weight[:, 2 * P * tile_n : 2 * P * (tile_n + 1)].bitcast(FP4X4),
+                    lhsT_scale=weight_scale[:, P * tile_n : P * (tile_n + 1)],
                     rhs=rhs.bitcast(FP8X4),
                     rhs_scale=rhs_scale,
                     start=True,
@@ -100,37 +107,34 @@ def tile_list_group_picks_and_context_kernel(
                 )
 
         context = {}
-        for h in range(2):
-            cols = slice(h * HALF, (h + 1) * HALF)
-            for m in range(2):
-                bank = psum.tile([P, 2, HALF], F32, name="q_bank%d%d" % (h, m))
-                product(bank, wc_codes, wc_scale, m, cx_codes[:, cols], cx_scale[:, cols])
-                context[h, m] = keep.tile([P, 2, HALF], F32, name="context%d%d" % (h, m))
-                nc.scalar.copy(out=context[h, m][:], in_=bank[:])
-
         banks = {}
         for h in range(2):
-            grouped = keep.tile([P, HALF * PACK], BF16, name="grouped%d" % h, align_bytes=64)
-            nc.vector.tensor_copy(
-                out=grouped[:].bitcast(I32).rearrange("p (c u) -> p c u", u=2),
-                in_=pairs[h][:].rearrange("p u c e -> p u (c e)").bitcast(I32).rearrange("p u c -> p c u"),
-            )
-            xs_codes = keep.tile([P, HALF], U32, name="xs_codes%d" % h, align_bytes=64)
-            xs_scale = keep.tile([P, HALF], U8, name="xs_scale%d" % h, align_bytes=64)
-            nc.vector.quantize_mx(out=xs_codes[:].bitcast(FP8X4), scales=xs_scale[:], in_=grouped[:])
+            for m in range(2):
+                bank = psum.tile([P, 2, HALF], F32, name="q_bank%d%d" % (h, m))
+                product(bank, wc_codes, wc_scale, m, cx_codes[h], cx_scale[:, h * HALF : (h + 1) * HALF])
+                context[h, m] = keep.tile([P, 2, HALF], F32, name="context%d%d" % (h, m))
+                nc.scalar.copy(out=context[h, m][:], in_=bank[:])
+        for h in range(2):
             for m in range(2):
                 banks[h, m] = psum.tile([P, 2, HALF], F32, name="p_bank%d%d" % (h, m))
-                product(banks[h, m], w_codes, w_scale, m, xs_codes[:], xs_scale[:])
+                product(banks[h, m], w_codes, w_scale, m, xs_codes[h][:], xs_scale[h][:])
 
         for h in range(2):
             for m in range(2):
-                result = keep.tile([P, 2, HALF], F32, name="result%d%d" % (h, m))
-                nc.vector.scalar_tensor_tensor(
-                    out=result[:], in0=banks[h, m][:], scalar=0.0, in1=context[h, m][:], op0=MAX, op1=ADD
-                )
-                nc.sync.dma_start(
-                    out=out[2 * P * m : 2 * P * (m + 1), h * HALF : (h + 1) * HALF].rearrange(
-                        "(s p) j -> p s j", s=2
-                    ),
-                    in_=result[:],
-                )
+                pieces = [(0, 1), (1, 2)] if h == m else [(0, 2)]
+                for s0, s1 in pieces:
+                    result = keep.tile([P, s1 - s0, HALF], F32, name="result%d%d%d" % (h, m, s0))
+                    nc.vector.scalar_tensor_tensor(
+                        out=result[:],
+                        in0=banks[h, m][:, s0:s1, :],
+                        scalar=0.0,
+                        in1=context[h, m][:, s0:s1, :],
+                        op0=MAX,
+                        op1=ADD,
+                    )
+                    nc.sync.dma_start(
+                        out=out[P * (2 * m + s0) : P * (2 * m + s1), h * HALF : (h + 1) * HALF].rearrange(
+                            "(s p) j -> p s j", p=P
+                        ),
+                        in_=result[:],
+                    )

from contextlib import ExitStack

import concourse.mybir as mybir

K, T, J, L, N = 512, 1024, 512, 512, 512
FLOPS = 2 * K * N * J + 2 * L * N * J

F32 = mybir.dt.float32
BF16 = mybir.dt.bfloat16
I32 = mybir.dt.int32
U32 = mybir.dt.uint32
U16 = mybir.dt.uint16
U8 = mybir.dt.uint8
FP8X4 = mybir.dt.float8_e4m3fn_x4
FP4X4 = mybir.dt.float4_e2m1fn_x4
COPY = mybir.ActivationFunctionType.Copy
MAX = mybir.AluOpType.max
ADD = mybir.AluOpType.add

P = 128
PACK = 4
HALF = J // 2
LIST_COLS = HALF // 16


def tile_list_group_picks_and_context_kernel(
    tc, xf, fk, w_words, w_scales, cx_words, cx_scales, wc_words, wc_scales, offs, out
):
    nc = tc.nc
    with ExitStack() as ctx:
        keep = ctx.enter_context(tc.tile_pool(name="keep", bufs=1))
        psum = ctx.enter_context(tc.psum_pool(name="psum", bufs=1))

        offsets = keep.tile([P, J // 16], U16, name="offsets")
        factor = keep.tile([P, PACK], F32, name="factor")
        planes = [keep.tile([P, T], F32, name="plane%d" % t) for t in range(PACK)]
        scale_rows = keep.tile([16, N + J + N], U8, name="scale_rows")
        scales = keep.tile([P, N + J + N], U8, name="scales", align_bytes=64)
        wc_cols, cx_cols, w_cols = slice(0, N), slice(N, N + J), slice(N + J, N + J + N)
        wc_scale, cx_scale, w_scale = scales[:, wc_cols], scales[:, cx_cols], scales[:, w_cols]
        nc.vector.memset(scales[:].bitcast(I32), 0)
        warm = keep.tile([P, 8], F32, name="warm")
        warm2 = keep.tile([P, 8], F32, name="warm2")
        nc.vector.memset(warm[:], 0.0)
        nc.scalar.activation(out=warm2[:], in_=warm[:], func=COPY)

        xf_rows = xf.rearrange("(p t) c -> p t c", t=PACK)
        nc.sync.dma_start(out=planes[0][:], in_=xf_rows[:, 0, :])
        nc.sync.dma_start(offsets[:], offs)
        nc.sync.dma_start(out=factor[:], in_=fk.rearrange("(p t) o -> p (t o)", t=PACK))
        for cols, rows in ((wc_cols, wc_scales), (cx_cols, cx_scales), (w_cols, w_scales)):
            nc.sync.dma_start(out=scale_rows[:, cols].bitcast(I32), in_=rows[0].bitcast(I32))
        for t in range(1, PACK):
            nc.sync.dma_start(out=planes[t][:], in_=xf_rows[:, t, :])
        for quad in range(4):
            nc.sync.dma_start(
                out=scales[32 * quad : 32 * quad + 4, :].bitcast(I32),
                in_=scale_rows[4 * quad : 4 * quad + 4, :].bitcast(I32),
            )

        pairs = [keep.tile([P, 2, HALF, 2], BF16, name="pairs%d" % h) for h in range(2)]

        def scale_and_round(picked, t, h):
            nc.scalar.activation(
                out=pairs[h][:, t // 2, :, t % 2], in_=picked, func=COPY, scale=factor[:, t : t + 1]
            )

        for t in range(PACK):
            for h in range(2):
                picked = keep.tile([P, HALF], F32, name="picked%d%d" % (t, h), align_bytes=64)
                nc.vector.tensor_copy(
                    picked[:], planes[t][:].indirect(offsets[:, h * LIST_COLS : (h + 1) * LIST_COLS])
                )
                scale_and_round(picked[:], t, h)

        xs_codes, xs_scale = {}, {}
        for h in range(2):
            grouped = keep.tile([P, HALF * PACK], BF16, name="grouped%d" % h, align_bytes=64)
            nc.vector.tensor_copy(
                out=grouped[:].bitcast(F32).rearrange("p (c i u) -> p c u i", i=4, u=2),
                in_=pairs[h][:].rearrange("p u c e -> p u (c e)").bitcast(F32).rearrange("p u (c i) -> p c u i", i=4),
            )
            xs_codes[h] = keep.tile([P, HALF], U32, name="xs_codes%d" % h, align_bytes=64)
            xs_scale[h] = keep.tile([P, HALF], U8, name="xs_scale%d" % h, align_bytes=64)
            nc.vector.quantize_mx(out=xs_codes[h][:].bitcast(FP8X4), scales=xs_scale[h][:], in_=grouped[:])

        codes = keep.tile([P, 2 * N + 4 * J + 2 * N], U8, name="codes", tag="picked00", align_bytes=64)
        wc_codes, w_codes = codes[:, 0 : 2 * N], codes[:, 2 * N : 4 * N]
        cx_codes = [codes[:, 4 * N + 4 * HALF * h : 4 * N + 4 * HALF * (h + 1)] for h in range(2)]
        cx_rows = cx_words[0].rearrange("p c r -> p (c r)")
        nc.sync.dma_start(out=wc_codes.bitcast(I32), in_=wc_words[0].bitcast(I32))
        nc.sync.dma_start(out=cx_codes[0].bitcast(I32), in_=cx_rows[:, 0 : 4 * HALF].bitcast(I32))
        nc.sync.dma_start(out=cx_codes[1].bitcast(I32), in_=cx_rows[:, 4 * HALF : 4 * J].bitcast(I32))
        nc.sync.dma_start(out=w_codes.bitcast(I32), in_=w_words[0].bitcast(I32))

        def product(bank, weight, weight_scale, m, rhs, rhs_scale):
            for s in range(2):
                tile_n = 2 * m + s
                nc.tensor.matmul_mx(
                    out=bank[:, s, :],
                    lhsT=weight[:, 2 * P * tile_n : 2 * P * (tile_n + 1)].bitcast(FP4X4),
                    lhsT_scale=weight_scale[:, P * tile_n : P * (tile_n + 1)],
                    rhs=rhs.bitcast(FP8X4),
                    rhs_scale=rhs_scale,
                    start=True,
                    stop=True,
                )

        context = {}
        banks = {}
        for h in range(2):
            for m in range(2):
                bank = psum.tile([P, 2, HALF], F32, name="q_bank%d%d" % (h, m))
                product(bank, wc_codes, wc_scale, m, cx_codes[h], cx_scale[:, h * HALF : (h + 1) * HALF])
                context[h, m] = keep.tile([P, 2, HALF], F32, name="context%d%d" % (h, m))
                nc.scalar.copy(out=context[h, m][:], in_=bank[:])
        for h in range(2):
            for m in range(2):
                banks[h, m] = psum.tile([P, 2, HALF], F32, name="p_bank%d%d" % (h, m))
                product(banks[h, m], w_codes, w_scale, m, xs_codes[h][:], xs_scale[h][:])

        for h in range(2):
            for m in range(2):
                pieces = [(0, 1), (1, 2)] if h == m else [(0, 2)]
                for s0, s1 in pieces:
                    result = keep.tile([P, s1 - s0, HALF], F32, name="result%d%d%d" % (h, m, s0))
                    nc.vector.scalar_tensor_tensor(
                        out=result[:],
                        in0=banks[h, m][:, s0:s1, :],
                        scalar=0.0,
                        in1=context[h, m][:, s0:s1, :],
                        op0=MAX,
                        op1=ADD,
                    )
                    nc.sync.dma_start(
                        out=out[P * (2 * m + s0) : P * (2 * m + s1), h * HALF : (h + 1) * HALF].rearrange(
                            "(s p) j -> p s j", p=P
                        ),
                        in_=result[:],
                    )
